import numpy as np
import ml_dtypes


def mxq(x, axis, fmt="e4m3"):
    dtype, down = {"e4m3": (ml_dtypes.float8_e4m3fn, 7), "e5m2": (ml_dtypes.float8_e5m2, 14)}[fmt]
    v = np.moveaxis(np.asarray(x, np.float32).astype(ml_dtypes.bfloat16).astype(np.float64), axis, -1)
    blocks = v.reshape(v.shape[:-1] + (-1, 32))
    amax = np.abs(blocks).max(-1, keepdims=True)
    byte = np.maximum(np.where(amax > 0, np.frexp(amax)[1] - 1 + 127, 0) - down, 1)
    scale = np.exp2(byte - 127.0)
    codes = (blocks / scale).astype(np.float32).astype(dtype).astype(np.float64)
    return np.moveaxis((codes * scale).reshape(v.shape), -1, axis)


WIDE = False


def mx_kscale(k):
    if not WIDE:
        return np.ones(k)
    levels = np.array([10, -10, 5, -5, 0])
    if k % 512:
        return np.exp2(np.random.permutation(np.resize(levels, k // 32))).repeat(32)
    a = np.empty((k // 512, 16))
    for p in range(k // 512):
        a[p, :8] = np.random.permutation(np.resize(levels, 8))
        for g in range(8):
            far = levels[np.abs(levels - a[p, g]) >= 10]
            a[p, g + 8] = far[np.random.randint(len(far))]
    return np.exp2(a.ravel()).repeat(32)


def f64(x):
    return np.asarray(x).astype(np.float64)


def striped(idx):
    return np.tile(idx.reshape(-1, 16).T, (8, 1)).astype(np.uint16)


def unstriped(offs):
    return offs[:16].T.reshape(-1).astype(np.int64)


def pack_weight(w):
    k, n = w.shape
    w = f64(np.asarray(w, np.float32).astype(ml_dtypes.bfloat16)).reshape(k // 32, 32, n)
    amax = np.abs(w).max(1)
    byte = np.clip(np.where(amax > 0, np.frexp(amax)[1] - 1 + 127 - 7, 1), 1, 254)
    scaled = (w * np.exp2(127.0 - byte)[:, None, :]).reshape(k, n).astype(np.float32)
    words = np.ascontiguousarray(scaled.reshape(k // 512, 128, 4, n).transpose(0, 1, 3, 2)).astype(ml_dtypes.float8_e4m3fn).view(np.uint8)
    return words, np.ascontiguousarray(byte.astype(np.uint8).reshape(k // 512, 16, n))


def unpack_weight(words, scales):
    g, p, n, _ = words.shape
    vals = np.ascontiguousarray(words).view(ml_dtypes.float8_e4m3fn).astype(np.float64) * np.repeat(np.exp2(scales.astype(np.float64) - 127.0), 8, axis=1)[..., None]
    return vals.transpose(0, 1, 3, 2).reshape(g * 512, n)


def relu(v):
    return np.maximum(v, 0.0)

def planes(y):
    n, m = y.shape
    v = y.astype(np.float32).astype(ml_dtypes.bfloat16).astype(np.float64).reshape(n // 32, 32, m)
    top = np.abs(v).max(1)
    byte = np.clip(np.where(top > 0, np.frexp(top)[1] - 1 + 127 - 7, 1), 1, 254)
    codes = (v * np.exp2(127.0 - byte)[:, None, :]).reshape(n, m).astype(np.float32).astype(ml_dtypes.float8_e4m3fn).view(np.uint8)
    words = codes.reshape(n // 512, 128, 4, m).transpose(0, 1, 3, 2)
    return np.ascontiguousarray(words), np.ascontiguousarray(byte.astype(np.uint8).reshape(n // 512, 16, m))


K, T, N = 512, 512, 512


def setup_inputs():
    n = np.random.standard_normal
    s = mx_kscale(K)[:, None]
    packed_xT = pack_weight(n((K, T)) * s)
    return {
        "x_words": packed_xT[0],
        "x_scales": packed_xT[1],
        "w1": (n((K, N)) / np.sqrt(K) / s).astype(np.float32),
        "w2": (n((K, N)) / np.sqrt(K) / s).astype(np.float32),
        "w3": (n((K, N)) / np.sqrt(K) / s).astype(np.float32),
        "pos1": striped(np.random.permutation(T)),
        "pos2": striped(np.random.permutation(T)),
        "pos3": striped(np.random.permutation(T)),
    }


def reference(x_words, x_scales, w1, w2, w3, pos1, pos2, pos3):
    xq = unpack_weight(x_words, x_scales)
    h = mxq(f64(w3), 0, "e4m3").T @ xq
    g = mxq(f64(w1), 0, "e4m3").T @ xq
    s = mxq(f64(w2), 0, "e4m3").T @ xq
    out_0 = relu(h[:, unstriped(pos1)] * g + s) + relu(h[:, unstriped(pos2)] * g + s) + relu(h[:, unstriped(pos3)] * g + s)
    return (out_0,) + planes(out_0)

@@ -1,0 +1,186 @@
+from contextlib import ExitStack
+
+import concourse.mybir as mybir
+from concourse.masks import make_identity
+
+K, T, N = 512, 512, 512
+FLOPS = 3 * 2 * K * T * N
+
+F32 = mybir.dt.float32
+BF16 = mybir.dt.bfloat16
+I32 = mybir.dt.int32
+U32 = mybir.dt.uint32
+U16 = mybir.dt.uint16
+U8 = mybir.dt.uint8
+FP8X4 = mybir.dt.float8_e4m3fn_x4
+ALU = mybir.AluOpType
+RELU = mybir.ActivationFunctionType.Relu
+
+P = 128
+PACK = 4
+HALF = N // 2
+BLK = 128
+WIDE = 384
+
+
+def tile_picked_wfilmg_relu_lo_kernel(
+    tc, x_words, x_scales, w1, w2, w3, pos1, pos2, pos3, out_0, out_1, out_2
+):
+    nc = tc.nc
+    with ExitStack() as ctx:
+        keep = ctx.enter_context(tc.tile_pool(name="keep", bufs=1))
+        alias = ctx.enter_context(tc.tile_pool(name="alias", bufs=1))
+        psum = ctx.enter_context(tc.psum_pool(name="psum", bufs=1))
+
+        x_sc = keep.tile([P, T], U8, name="x_sc", align_bytes=64)
+        nc.gpsimd.memset(x_sc[:].bitcast(I32), 0)
+        for q in range(4):
+            nc.scalar.dma_start(out=x_sc[32 * q : 32 * q + 4, :].bitcast(I32), in_=x_scales[0, 4 * q : 4 * q + 4, :].bitcast(I32))
+
+        def load_w(w, label):
+            rows = w.rearrange("(p j) c -> p j c", j=PACK)
+            halves = []
+            for a in range(2):
+                raw = keep.tile([P, PACK, HALF], F32, name=f"raw_{label}{a}")
+                nc.sync.dma_start(out=raw[:], in_=rows[:, :, a * HALF : (a + 1) * HALF])
+                halves.append(raw)
+            return halves
+
+        raw_h = load_w(w3, "h")
+        x_cd = keep.tile([P, T], U32, name="x_cd", align_bytes=64)
+        nc.sync.dma_start(out=x_cd[:].bitcast(I32), in_=x_words[0].rearrange("p n r -> p (n r)").bitcast(I32))
+        raw_g = load_w(w1, "g")
+        lists = []
+        for d, pos in enumerate((pos1, pos2, pos3)):
+            offsets = keep.tile([P, T // 16], U16, name=f"offsets{d}")
+            nc.sync.dma_start(offsets[:], pos)
+            lists.append(offsets)
+        raw_s = load_w(w2, "s")
+
+        ident_raw = keep.tile([P, P], F32, name="ident_raw")
+        make_identity(nc, ident_raw[:])
+        ident = keep.tile([P, P], F32, name="ident")
+        nc.scalar.activation(ident[:], ident_raw[:], RELU)
+
+        def deal(engine_copy, grouped, raw, a, m0, m1):
+            dst = grouped[:].rearrange("p (t m j) -> p m j t", t=PACK, j=PACK)
+            src = raw[:].rearrange("p j (m t) -> p m j t", t=PACK)
+            base = a * (HALF // PACK)
+            engine_copy(out=dst[:, base + m0 : base + m1], in_=src[:, m0:m1])
+
+        def quantise(grouped, label, spans):
+            res = []
+            for t0, t1 in spans:
+                width = (t1 - t0) * P
+                cd = keep.tile([P, width], U32, name=f"cd_{label}{t0}", align_bytes=64)
+                sc = keep.tile([P, width], U8, name=f"sc_{label}{t0}", align_bytes=64)
+                nc.vector.quantize_mx(out=cd[:].bitcast(FP8X4), scales=sc[:], in_=grouped[:, t0 * P * PACK : t1 * P * PACK])
+                for i in range(t1 - t0):
+                    res.append((cd[:, i * P : (i + 1) * P], sc[:, i * P : (i + 1) * P]))
+            return res
+
+        def project(wq, t, dst, copy_out=nc.scalar.copy):
+            acc = psum.tile([P, T], F32, name="acc", tag="acc", bufs=3)
+            nc.tensor.matmul_mx(out=acc[:], lhsT=wq[t][0].bitcast(FP8X4), lhsT_scale=wq[t][1],
+                                rhs=x_cd[:].bitcast(FP8X4), rhs_scale=x_sc[:], start=True, stop=True)
+            copy_out(out=dst, in_=acc[:])
+
+        grouped_h = keep.tile([P, N * PACK], BF16, name="grouped_h", align_bytes=64)
+        grouped_g = keep.tile([P, N * PACK], BF16, name="grouped_g", align_bytes=64)
+        grouped_s = alias.tile([P, N * PACK], BF16, name="grouped_s", align_bytes=64, offset=0)
+        h = [keep.tile([P, T], F32, name=f"h{t}") for t in range(PACK)]
+        g = [keep.tile([P, T], F32, name=f"g{t}") for t in range(PACK)]
+        s = keep.tile([P, PACK, T], F32, name="s")
+
+        for a in range(2):
+            deal(nc.vector.tensor_copy, grouped_h, raw_h[a], a, 0, 64)
+        wq_h = quantise(grouped_h, "h", [(0, 1), (1, 2), (2, 4)])
+        project(wq_h, 0, h[0][:])
+        deal(nc.vector.tensor_copy, grouped_g, raw_g[0], 0, 0, 64)
+        deal(nc.vector.tensor_copy, grouped_g, raw_g[1], 1, 0, 44)
+        deal(nc.scalar.copy, grouped_g, raw_g[1], 1, 44, 64)
+        wq_g = quantise(grouped_g, "g", [(0, 1), (1, 2), (2, 4)])
+        project(wq_g, 0, g[0][:], nc.vector.tensor_copy)
+        deal(nc.scalar.copy, grouped_s, raw_s[0], 0, 0, 64)
+        deal(nc.scalar.copy, grouped_s, raw_s[1], 1, 0, 64)
+        wq_s = quantise(grouped_s, "s", [(0, 2), (2, 4)])
+
+        out_rows = out_0.rearrange("(p t) v -> p t v", t=PACK)
+        y_sc = keep.tile([P, T], U8, name="y_sc", align_bytes=64)
+        words_out = out_1[0].rearrange("p n r -> p (n r)").bitcast(I32)
+
+        def add_transposed(bank, parts):
+            for i, (cols, block) in enumerate(parts):
+                nc.tensor.matmul(bank[:, cols], lhsT=block, rhs=ident[:], is_transpose=True,
+                                 start=(i == 0), stop=(i == len(parts) - 1))
+
+        def blk(i):
+            return slice(i * BLK, (i + 1) * BLK)
+
+        def planes(engine_copy, y, c0, width, v0, label):
+            rounded = keep.tile([P, width * PACK], BF16, name=f"rounded{label}", align_bytes=64)
+            engine_copy(out=rounded[:].rearrange("p (c i t) -> p c t i", i=4, t=PACK),
+                        in_=y[:, :, c0 : c0 + width].rearrange("p t (c i) -> p c t i", i=4))
+            words = keep.tile([P, width], U32, name=f"words{label}", align_bytes=64)
+            nc.vector.quantize_mx(out=words[:].bitcast(FP8X4), scales=y_sc[:, v0 : v0 + width], in_=rounded[:])
+            nc.sync.dma_start(out=words_out[:, v0 : v0 + width], in_=words[:].bitcast(I32))
+
+        nb = WIDE // BLK
+        behind_s = {(0, 2): 0, (1, 0): WIDE * 4, (1, 1): WIDE * 8}
+        y_wide = keep.tile([P, PACK, WIDE], F32, name="y_wide")
+        for t in range(PACK):
+            u = []
+            for d in range(3):
+                if (t, d) in behind_s:
+                    ud = alias.tile([P, WIDE], F32, name=f"u{t}_{d}", offset=behind_s[(t, d)])
+                else:
+                    ud = keep.tile([P, WIDE], F32, name=f"u{d}", tag=f"u{d}", bufs=1 if d < 2 else 2)
+                nc.vector.tensor_tensor(ud[:], h[t][:].indirect(lists[d][:, 0 : WIDE // 16]), g[t][:, 0:WIDE], ALU.mult)
+                u.append(ud)
+            if t + 1 < PACK:
+                project(wq_h, t + 1, h[t + 1][:])
+                project(wq_g, t + 1, g[t + 1][:])
+            project(wq_s, t, s[:, t, :])
+            r = []
+            for d in range(2):
+                fwd = psum.tile([P, T], F32, name="fwd", tag="fwd", bufs=3)
+                add_transposed(fwd, [(blk(b), s[:, t, blk(b)]) for b in range(nb)] + [(blk(b), u[d][:, blk(b)]) for b in range(nb)])
+                rd = keep.tile([P, WIDE], F32, name=f"r{t}_{d}")
+                nc.scalar.activation(rd[:], fwd[:, 0:WIDE], RELU)
+                r.append(rd)
+            back = psum.tile([P, T], F32, name="back", tag="back", bufs=2)
+            add_transposed(back, [(blk(b), r[d][:, blk(b)]) for d in range(2) for b in range(nb)])
+            pre = alias.tile([P, WIDE], F32, name=f"pre{t}", offset=8192 + 1280)
+            nc.vector.tensor_tensor(pre[:], u[2][:], s[:, t, 0:WIDE], ALU.add)
+            nc.vector.scalar_tensor_tensor(y_wide[:, t, :], pre[:], 0.0, back[:, 0:WIDE], ALU.max, ALU.add)
+            nc.sync.dma_start(out=out_rows[:, t, 0:WIDE], in_=y_wide[:, t, :])
+
+        u = []
+        for d in range(3):
+            if d == 0:
+                ud = keep.tile([P, PACK, BLK], F32, name="u0", tag="u0", bufs=1)
+            else:
+                ud = alias.tile([P, PACK, BLK], F32, name=f"ul_{d}", offset=8192 + (d - 1) * 2048)
+            for t in range(PACK):
+                nc.vector.tensor_tensor(ud[:, t, :], h[t][:].indirect(lists[d][:, WIDE // 16 : T // 16]), g[t][:, WIDE:T], ALU.mult)
+            u.append(ud)
+        r = []
+        for d in range(2):
+            fwd = psum.tile([P, T], F32, name="fwd", tag="fwd", bufs=3)
+            add_transposed(fwd, [(blk(t), s[:, t, WIDE:T]) for t in range(PACK)] + [(blk(t), u[d][:, t, :]) for t in range(PACK)])
+            rd = keep.tile([P, T], F32, name=f"rl_{d}")
+            nc.scalar.activation(rd[:], fwd[:], RELU)
+            r.append(rd)
+        planes(nc.scalar.copy, y_wide, 0, 256, 0, "a")
+        planes(nc.scalar.copy, y_wide, 256, 128, 256, "b")
+        back = psum.tile([P, T], F32, name="back", tag="back", bufs=2)
+        add_transposed(back, [(blk(t), r[d][:, blk(t)]) for d in range(2) for t in range(PACK)])
+        pre = keep.tile([P, PACK, BLK], F32, name="prel")
+        nc.vector.tensor_tensor(pre[:], u[2][:], s[:, :, WIDE:T], ALU.add)
+        y_last = keep.tile([P, PACK, BLK], F32, name="y_last")
+        nc.vector.scalar_tensor_tensor(y_last[:].rearrange("p t c -> p (t c)"), pre[:].rearrange("p t c -> p (t c)"), 0.0, back[:], ALU.max, ALU.add)
+        nc.sync.dma_start(out=out_rows[:, :, WIDE:T], in_=y_last[:])
+        planes(nc.vector.tensor_copy, y_last, 0, BLK, WIDE, "c")
+        for q in range(4):
+            queue = nc.scalar if q % 2 else nc.sync
+            queue.dma_start(out=out_2[0, 4 * q : 4 * q + 4, :].bitcast(I32), in_=y_sc[32 * q : 32 * q + 4, :].bitcast(I32))

@@ -21,6 +21,7 @@ PACK = 4
 HALF = N // 2
 BLK = 128
 WIDE = 384
+ALL_TENSOR = (0, 1, 2)
 
 
 def tile_picked_wfilmg_relu_lo_kernel(
@@ -94,15 +95,14 @@ def tile_picked_wfilmg_relu_lo_kernel(
 
         for a in range(2):
             deal(nc.vector.tensor_copy, grouped_h, raw_h[a], a, 0, 64)
-        wq_h = quantise(grouped_h, "h", [(0, 1), (1, 2), (2, 4)])
+        wq_h = quantise(grouped_h, "h", [(0, 4)])
         project(wq_h, 0, h[0][:])
         deal(nc.vector.tensor_copy, grouped_g, raw_g[0], 0, 0, 64)
-        deal(nc.vector.tensor_copy, grouped_g, raw_g[1], 1, 0, 44)
-        deal(nc.scalar.copy, grouped_g, raw_g[1], 1, 44, 64)
+        deal(nc.vector.tensor_copy, grouped_g, raw_g[1], 1, 0, 64)
         wq_g = quantise(grouped_g, "g", [(0, 1), (1, 2), (2, 4)])
         project(wq_g, 0, g[0][:], nc.vector.tensor_copy)
         deal(nc.scalar.copy, grouped_s, raw_s[0], 0, 0, 64)
-        deal(nc.scalar.copy, grouped_s, raw_s[1], 1, 0, 64)
+        deal(nc.vector.tensor_copy, grouped_s, raw_s[1], 1, 0, 64)
         wq_s = quantise(grouped_s, "s", [(0, 2), (2, 4)])
 
         out_rows = out_0.rearrange("(p t) v -> p t v", t=PACK)
@@ -126,7 +126,8 @@ def tile_picked_wfilmg_relu_lo_kernel(
             nc.sync.dma_start(out=words_out[:, v0 : v0 + width], in_=words[:].bitcast(I32))
 
         nb = WIDE // BLK
-        behind_s = {(0, 2): 0, (1, 0): WIDE * 4, (1, 1): WIDE * 8}
+        turn = [0]
+        behind_s = {(0, 1): 0, (0, 2): WIDE * 4, (1, 0): WIDE * 8}
         y_wide = keep.tile([P, PACK, WIDE], F32, name="y_wide")
         for t in range(PACK):
             u = []
@@ -134,7 +135,7 @@ def tile_picked_wfilmg_relu_lo_kernel(
                 if (t, d) in behind_s:
                     ud = alias.tile([P, WIDE], F32, name=f"u{t}_{d}", offset=behind_s[(t, d)])
                 else:
-                    ud = keep.tile([P, WIDE], F32, name=f"u{d}", tag=f"u{d}", bufs=1 if d < 2 else 2)
+                    ud = keep.tile([P, WIDE], F32, name=f"u{d}", tag=f"u{d}", bufs=2)
                 nc.vector.tensor_tensor(ud[:], h[t][:].indirect(lists[d][:, 0 : WIDE // 16]), g[t][:, 0:WIDE], ALU.mult)
                 u.append(ud)
             if t + 1 < PACK:
@@ -142,23 +143,30 @@ def tile_picked_wfilmg_relu_lo_kernel(
                 project(wq_g, t + 1, g[t + 1][:])
             project(wq_s, t, s[:, t, :])
             r = []
-            for d in range(2):
-                fwd = psum.tile([P, T], F32, name="fwd", tag="fwd", bufs=3)
-                add_transposed(fwd, [(blk(b), s[:, t, blk(b)]) for b in range(nb)] + [(blk(b), u[d][:, blk(b)]) for b in range(nb)])
+            by_tensor = 3 if t in ALL_TENSOR else 2
+            for d in range(by_tensor):
+                fwd = psum.tile([P, T], F32, name=f"fwd{turn[0] % 3}", tag=f"fwd{turn[0] % 3}", bufs=1)
+                turn.append(turn.pop() + 1)
+                shift_parts = [(blk(b), s[:, t, blk(b)]) for b in range(nb)]
+                term_parts = [(blk(b), u[d][:, blk(b)]) for b in range(nb)]
+                add_transposed(fwd, term_parts + shift_parts if t == 0 else shift_parts + term_parts)
                 rd = keep.tile([P, WIDE], F32, name=f"r{t}_{d}")
                 nc.scalar.activation(rd[:], fwd[:, 0:WIDE], RELU)
                 r.append(rd)
             back = psum.tile([P, T], F32, name="back", tag="back", bufs=2)
-            add_transposed(back, [(blk(b), r[d][:, blk(b)]) for d in range(2) for b in range(nb)])
-            pre = alias.tile([P, WIDE], F32, name=f"pre{t}", offset=8192 + 1280)
-            nc.vector.tensor_tensor(pre[:], u[2][:], s[:, t, 0:WIDE], ALU.add)
-            nc.vector.scalar_tensor_tensor(y_wide[:, t, :], pre[:], 0.0, back[:, 0:WIDE], ALU.max, ALU.add)
+            add_transposed(back, [(blk(b), r[d][:, blk(b)]) for d in range(by_tensor) for b in range(nb)])
+            if by_tensor == 3:
+                nc.scalar.copy(out=y_wide[:, t, :], in_=back[:, 0:WIDE])
+            else:
+                pre = alias.tile([P, WIDE], F32, name=f"pre{t}", offset=8192 + 1280 if t == PACK - 1 else 16384)
+                nc.vector.tensor_tensor(pre[:], u[2][:], s[:, t, 0:WIDE], ALU.add)
+                nc.vector.scalar_tensor_tensor(y_wide[:, t, :], pre[:], 0.0, back[:, 0:WIDE], ALU.max, ALU.add)
             nc.sync.dma_start(out=out_rows[:, t, 0:WIDE], in_=y_wide[:, t, :])
 
         u = []
         for d in range(3):
             if d == 0:
-                ud = keep.tile([P, PACK, BLK], F32, name="u0", tag="u0", bufs=1)
+                ud = keep.tile([P, PACK, BLK], F32, name="u0", tag="u0", bufs=2)
             else:
                 ud = alias.tile([P, PACK, BLK], F32, name=f"ul_{d}", offset=8192 + (d - 1) * 2048)
             for t in range(PACK):
@@ -166,7 +174,8 @@ def tile_picked_wfilmg_relu_lo_kernel(
             u.append(ud)
         r = []
         for d in range(2):
-            fwd = psum.tile([P, T], F32, name="fwd", tag="fwd", bufs=3)
+            bank = (turn[0] - 1 - d) % 3
+            fwd = psum.tile([P, T], F32, name=f"fwd{bank}", tag=f"fwd{bank}", bufs=1)
             add_transposed(fwd, [(blk(t), s[:, t, WIDE:T]) for t in range(PACK)] + [(blk(t), u[d][:, t, :]) for t in range(PACK)])
             rd = keep.tile([P, T], F32, name=f"rl_{d}")
             nc.scalar.activation(rd[:], fwd[:], RELU)
@@ -176,9 +185,12 @@ def tile_picked_wfilmg_relu_lo_kernel(
         back = psum.tile([P, T], F32, name="back", tag="back", bufs=2)
         add_transposed(back, [(blk(t), r[d][:, blk(t)]) for d in range(2) for t in range(PACK)])
         pre = keep.tile([P, PACK, BLK], F32, name="prel")
-        nc.vector.tensor_tensor(pre[:], u[2][:], s[:, :, WIDE:T], ALU.add)
         y_last = keep.tile([P, PACK, BLK], F32, name="y_last")
-        nc.vector.scalar_tensor_tensor(y_last[:].rearrange("p t c -> p (t c)"), pre[:].rearrange("p t c -> p (t c)"), 0.0, back[:], ALU.max, ALU.add)
+        back_t = back[:].rearrange("p (t c) -> p t c", t=PACK)
+        for t0, t1 in ((0, 3), (3, 4)):
+            nc.vector.tensor_tensor(pre[:, t0:t1], u[2][:, t0:t1], s[:, t0:t1, WIDE:T], ALU.add)
+        for t0, t1 in ((0, 3), (3, 4)):
+            nc.vector.scalar_tensor_tensor(y_last[:, t0:t1], pre[:, t0:t1], 0.0, back_t[:, t0:t1], ALU.max, ALU.add)
         nc.sync.dma_start(out=out_rows[:, :, WIDE:T], in_=y_last[:])
         planes(nc.vector.tensor_copy, y_last, 0, BLK, WIDE, "c")
         for q in range(4):

@@ -21,7 +21,7 @@ PACK = 4
 HALF = N // 2
 BLK = 128
 WIDE = 384
-ALL_TENSOR = (0, 1, 2)
+BY_TENSOR = (0, 3, 2, 2)
 
 
 def tile_picked_wfilmg_relu_lo_kernel(
@@ -35,8 +35,6 @@ def tile_picked_wfilmg_relu_lo_kernel(
 
         x_sc = keep.tile([P, T], U8, name="x_sc", align_bytes=64)
         nc.gpsimd.memset(x_sc[:].bitcast(I32), 0)
-        for q in range(4):
-            nc.scalar.dma_start(out=x_sc[32 * q : 32 * q + 4, :].bitcast(I32), in_=x_scales[0, 4 * q : 4 * q + 4, :].bitcast(I32))
 
         def load_w(w, label):
             rows = w.rearrange("(p j) c -> p j c", j=PACK)
@@ -45,18 +43,20 @@ def tile_picked_wfilmg_relu_lo_kernel(
                 raw = keep.tile([P, PACK, HALF], F32, name=f"raw_{label}{a}")
                 nc.sync.dma_start(out=raw[:], in_=rows[:, :, a * HALF : (a + 1) * HALF])
                 halves.append(raw)
+                if label == "h" and a == 0:
+                    for q in range(4):
+                        nc.sync.dma_start(out=x_sc[32 * q : 32 * q + 4, :].bitcast(I32), in_=x_scales[0, 4 * q : 4 * q + 4, :].bitcast(I32))
             return halves
 
         raw_h = load_w(w3, "h")
         x_cd = keep.tile([P, T], U32, name="x_cd", align_bytes=64)
         nc.sync.dma_start(out=x_cd[:].bitcast(I32), in_=x_words[0].rearrange("p n r -> p (n r)").bitcast(I32))
         raw_g = load_w(w1, "g")
-        lists = []
-        for d, pos in enumerate((pos1, pos2, pos3)):
-            offsets = keep.tile([P, T // 16], U16, name=f"offsets{d}")
-            nc.sync.dma_start(offsets[:], pos)
-            lists.append(offsets)
+        lists = [keep.tile([P, T // 16], U16, name=f"offsets{d}") for d in range(3)]
+        nc.sync.dma_start(lists[0][:], pos1)
         raw_s = load_w(w2, "s")
+        nc.sync.dma_start(lists[1][:], pos2)
+        nc.sync.dma_start(lists[2][:], pos3)
 
         ident_raw = keep.tile([P, P], F32, name="ident_raw")
         make_identity(nc, ident_raw[:])
@@ -141,15 +141,28 @@ def tile_picked_wfilmg_relu_lo_kernel(
             if t + 1 < PACK:
                 project(wq_h, t + 1, h[t + 1][:])
                 project(wq_g, t + 1, g[t + 1][:])
-            project(wq_s, t, s[:, t, :])
+            if t + 1 < PACK:
+                project(wq_s, t + 1, s[:, t + 1, :])
+            if t == 0:
+                project(wq_s, 0, s[:, 0, :])
+                first = keep.tile([P, WIDE], F32, name="first")
+                total = keep.tile([P, WIDE], F32, name="total")
+                pres = [keep.tile([P, WIDE], F32, name=f"pre0_{d}") for d in range(3)]
+                for d in range(3):
+                    nc.vector.tensor_tensor(pres[d][:], u[d][:], s[:, 0, 0:WIDE], ALU.add)
+                nc.scalar.activation(first[:], pres[0][:], RELU)
+                nc.vector.scalar_tensor_tensor(total[:], pres[1][:], 0.0, first[:], ALU.max, ALU.add)
+                nc.vector.scalar_tensor_tensor(y_wide[:, 0, :], pres[2][:], 0.0, total[:], ALU.max, ALU.add)
+                nc.sync.dma_start(out=out_rows[:, 0, 0:WIDE], in_=y_wide[:, 0, :])
+                continue
             r = []
-            by_tensor = 3 if t in ALL_TENSOR else 2
+            by_tensor = BY_TENSOR[t]
             for d in range(by_tensor):
                 fwd = psum.tile([P, T], F32, name=f"fwd{turn[0] % 3}", tag=f"fwd{turn[0] % 3}", bufs=1)
                 turn.append(turn.pop() + 1)
                 shift_parts = [(blk(b), s[:, t, blk(b)]) for b in range(nb)]
                 term_parts = [(blk(b), u[d][:, blk(b)]) for b in range(nb)]
-                add_transposed(fwd, term_parts + shift_parts if t == 0 else shift_parts + term_parts)
+                add_transposed(fwd, term_parts + shift_parts if t == 1 else shift_parts + term_parts)
                 rd = keep.tile([P, WIDE], F32, name=f"r{t}_{d}")
                 nc.scalar.activation(rd[:], fwd[:, 0:WIDE], RELU)
                 r.append(rd)

from contextlib import ExitStack

import concourse.mybir as mybir
from concourse.masks import make_identity

K, T, N = 512, 512, 512
FLOPS = 3 * 2 * K * T * N

F32 = mybir.dt.float32
BF16 = mybir.dt.bfloat16
I32 = mybir.dt.int32
U32 = mybir.dt.uint32
U16 = mybir.dt.uint16
U8 = mybir.dt.uint8
FP8X4 = mybir.dt.float8_e4m3fn_x4
ALU = mybir.AluOpType
RELU = mybir.ActivationFunctionType.Relu

P = 128
PACK = 4
HALF = N // 2
BLK = 128
WIDE = 384
BY_TENSOR = (0, 3, 2, 2)


def tile_picked_wfilmg_relu_lo_kernel(
    tc, x_words, x_scales, w1, w2, w3, pos1, pos2, pos3, out_0, out_1, out_2
):
    nc = tc.nc
    with ExitStack() as ctx:
        keep = ctx.enter_context(tc.tile_pool(name="keep", bufs=1))
        alias = ctx.enter_context(tc.tile_pool(name="alias", bufs=1))
        psum = ctx.enter_context(tc.psum_pool(name="psum", bufs=1))

        x_sc = keep.tile([P, T], U8, name="x_sc", align_bytes=64)
        nc.gpsimd.memset(x_sc[:].bitcast(I32), 0)

        def load_w(w, label):
            rows = w.rearrange("(p j) c -> p j c", j=PACK)
            halves = []
            for a in range(2):
                raw = keep.tile([P, PACK, HALF], F32, name=f"raw_{label}{a}")
                nc.sync.dma_start(out=raw[:], in_=rows[:, :, a * HALF : (a + 1) * HALF])
                halves.append(raw)
                if label == "h" and a == 0:
                    for q in range(4):
                        nc.sync.dma_start(out=x_sc[32 * q : 32 * q + 4, :].bitcast(I32), in_=x_scales[0, 4 * q : 4 * q + 4, :].bitcast(I32))
            return halves

        raw_h = load_w(w3, "h")
        x_cd = keep.tile([P, T], U32, name="x_cd", align_bytes=64)
        nc.sync.dma_start(out=x_cd[:].bitcast(I32), in_=x_words[0].rearrange("p n r -> p (n r)").bitcast(I32))
        raw_g = load_w(w1, "g")
        lists = [keep.tile([P, T // 16], U16, name=f"offsets{d}") for d in range(3)]
        nc.sync.dma_start(lists[0][:], pos1)
        raw_s = load_w(w2, "s")
        nc.sync.dma_start(lists[1][:], pos2)
        nc.sync.dma_start(lists[2][:], pos3)

        ident_raw = keep.tile([P, P], F32, name="ident_raw")
        make_identity(nc, ident_raw[:])
        ident = keep.tile([P, P], F32, name="ident")
        nc.scalar.activation(ident[:], ident_raw[:], RELU)

        def deal(engine_copy, grouped, raw, a, m0, m1):
            dst = grouped[:].rearrange("p (t m j) -> p m j t", t=PACK, j=PACK)
            src = raw[:].rearrange("p j (m t) -> p m j t", t=PACK)
            base = a * (HALF // PACK)
            engine_copy(out=dst[:, base + m0 : base + m1], in_=src[:, m0:m1])

        def quantise(grouped, label, spans):
            res = []
            for t0, t1 in spans:
                width = (t1 - t0) * P
                cd = keep.tile([P, width], U32, name=f"cd_{label}{t0}", align_bytes=64)
                sc = keep.tile([P, width], U8, name=f"sc_{label}{t0}", align_bytes=64)
                nc.vector.quantize_mx(out=cd[:].bitcast(FP8X4), scales=sc[:], in_=grouped[:, t0 * P * PACK : t1 * P * PACK])
                for i in range(t1 - t0):
                    res.append((cd[:, i * P : (i + 1) * P], sc[:, i * P : (i + 1) * P]))
            return res

        def project(wq, t, dst, copy_out=nc.scalar.copy):
            acc = psum.tile([P, T], F32, name="acc", tag="acc", bufs=3)
            nc.tensor.matmul_mx(out=acc[:], lhsT=wq[t][0].bitcast(FP8X4), lhsT_scale=wq[t][1],
                                rhs=x_cd[:].bitcast(FP8X4), rhs_scale=x_sc[:], start=True, stop=True)
            copy_out(out=dst, in_=acc[:])

        grouped_h = keep.tile([P, N * PACK], BF16, name="grouped_h", align_bytes=64)
        grouped_g = keep.tile([P, N * PACK], BF16, name="grouped_g", align_bytes=64)
        grouped_s = alias.tile([P, N * PACK], BF16, name="grouped_s", align_bytes=64, offset=0)
        h = [keep.tile([P, T], F32, name=f"h{t}") for t in range(PACK)]
        g = [keep.tile([P, T], F32, name=f"g{t}") for t in range(PACK)]
        s = keep.tile([P, PACK, T], F32, name="s")

        for a in range(2):
            deal(nc.vector.tensor_copy, grouped_h, raw_h[a], a, 0, 64)
        wq_h = quantise(grouped_h, "h", [(0, 4)])
        project(wq_h, 0, h[0][:])
        deal(nc.vector.tensor_copy, grouped_g, raw_g[0], 0, 0, 64)
        deal(nc.vector.tensor_copy, grouped_g, raw_g[1], 1, 0, 64)
        wq_g = quantise(grouped_g, "g", [(0, 1), (1, 2), (2, 4)])
        project(wq_g, 0, g[0][:], nc.vector.tensor_copy)
        deal(nc.scalar.copy, grouped_s, raw_s[0], 0, 0, 64)
        deal(nc.vector.tensor_copy, grouped_s, raw_s[1], 1, 0, 64)
        wq_s = quantise(grouped_s, "s", [(0, 2), (2, 4)])

        out_rows = out_0.rearrange("(p t) v -> p t v", t=PACK)
        y_sc = keep.tile([P, T], U8, name="y_sc", align_bytes=64)
        words_out = out_1[0].rearrange("p n r -> p (n r)").bitcast(I32)

        def add_transposed(bank, parts):
            for i, (cols, block) in enumerate(parts):
                nc.tensor.matmul(bank[:, cols], lhsT=block, rhs=ident[:], is_transpose=True,
                                 start=(i == 0), stop=(i == len(parts) - 1))

        def blk(i):
            return slice(i * BLK, (i + 1) * BLK)

        def planes(engine_copy, y, c0, width, v0, label):
            rounded = keep.tile([P, width * PACK], BF16, name=f"rounded{label}", align_bytes=64)
            engine_copy(out=rounded[:].rearrange("p (c i t) -> p c t i", i=4, t=PACK),
                        in_=y[:, :, c0 : c0 + width].rearrange("p t (c i) -> p c t i", i=4))
            words = keep.tile([P, width], U32, name=f"words{label}", align_bytes=64)
            nc.vector.quantize_mx(out=words[:].bitcast(FP8X4), scales=y_sc[:, v0 : v0 + width], in_=rounded[:])
            nc.sync.dma_start(out=words_out[:, v0 : v0 + width], in_=words[:].bitcast(I32))

        nb = WIDE // BLK
        turn = [0]
        behind_s = {(0, 1): 0, (0, 2): WIDE * 4, (1, 0): WIDE * 8}
        y_wide = keep.tile([P, PACK, WIDE], F32, name="y_wide")
        for t in range(PACK):
            u = []
            for d in range(3):
                if (t, d) in behind_s:
                    ud = alias.tile([P, WIDE], F32, name=f"u{t}_{d}", offset=behind_s[(t, d)])
                else:
                    ud = keep.tile([P, WIDE], F32, name=f"u{d}", tag=f"u{d}", bufs=2)
                nc.vector.tensor_tensor(ud[:], h[t][:].indirect(lists[d][:, 0 : WIDE // 16]), g[t][:, 0:WIDE], ALU.mult)
                u.append(ud)
            if t + 1 < PACK:
                project(wq_h, t + 1, h[t + 1][:])
                project(wq_g, t + 1, g[t + 1][:])
            if t + 1 < PACK:
                project(wq_s, t + 1, s[:, t + 1, :])
            if t == 0:
                project(wq_s, 0, s[:, 0, :])
                first = keep.tile([P, WIDE], F32, name="first")
                total = keep.tile([P, WIDE], F32, name="total")
                pres = [keep.tile([P, WIDE], F32, name=f"pre0_{d}") for d in range(3)]
                for d in range(3):
                    nc.vector.tensor_tensor(pres[d][:], u[d][:], s[:, 0, 0:WIDE], ALU.add)
                nc.scalar.activation(first[:], pres[0][:], RELU)
                nc.vector.scalar_tensor_tensor(total[:], pres[1][:], 0.0, first[:], ALU.max, ALU.add)
                nc.vector.scalar_tensor_tensor(y_wide[:, 0, :], pres[2][:], 0.0, total[:], ALU.max, ALU.add)
                nc.sync.dma_start(out=out_rows[:, 0, 0:WIDE], in_=y_wide[:, 0, :])
                continue
            r = []
            by_tensor = BY_TENSOR[t]
            for d in range(by_tensor):
                fwd = psum.tile([P, T], F32, name=f"fwd{turn[0] % 3}", tag=f"fwd{turn[0] % 3}", bufs=1)
                turn.append(turn.pop() + 1)
                shift_parts = [(blk(b), s[:, t, blk(b)]) for b in range(nb)]
                term_parts = [(blk(b), u[d][:, blk(b)]) for b in range(nb)]
                add_transposed(fwd, term_parts + shift_parts if t == 1 else shift_parts + term_parts)
                rd = keep.tile([P, WIDE], F32, name=f"r{t}_{d}")
                nc.scalar.activation(rd[:], fwd[:, 0:WIDE], RELU)
                r.append(rd)
            back = psum.tile([P, T], F32, name="back", tag="back", bufs=2)
            add_transposed(back, [(blk(b), r[d][:, blk(b)]) for d in range(by_tensor) for b in range(nb)])
            if by_tensor == 3:
                nc.scalar.copy(out=y_wide[:, t, :], in_=back[:, 0:WIDE])
            else:
                pre = alias.tile([P, WIDE], F32, name=f"pre{t}", offset=8192 + 1280 if t == PACK - 1 else 16384)
                nc.vector.tensor_tensor(pre[:], u[2][:], s[:, t, 0:WIDE], ALU.add)
                nc.vector.scalar_tensor_tensor(y_wide[:, t, :], pre[:], 0.0, back[:, 0:WIDE], ALU.max, ALU.add)
            nc.sync.dma_start(out=out_rows[:, t, 0:WIDE], in_=y_wide[:, t, :])

        u = []
        for d in range(3):
            if d == 0:
                ud = keep.tile([P, PACK, BLK], F32, name="u0", tag="u0", bufs=2)
            else:
                ud = alias.tile([P, PACK, BLK], F32, name=f"ul_{d}", offset=8192 + (d - 1) * 2048)
            for t in range(PACK):
                nc.vector.tensor_tensor(ud[:, t, :], h[t][:].indirect(lists[d][:, WIDE // 16 : T // 16]), g[t][:, WIDE:T], ALU.mult)
            u.append(ud)
        r = []
        for d in range(2):
            bank = (turn[0] - 1 - d) % 3
            fwd = psum.tile([P, T], F32, name=f"fwd{bank}", tag=f"fwd{bank}", bufs=1)
            add_transposed(fwd, [(blk(t), s[:, t, WIDE:T]) for t in range(PACK)] + [(blk(t), u[d][:, t, :]) for t in range(PACK)])
            rd = keep.tile([P, T], F32, name=f"rl_{d}")
            nc.scalar.activation(rd[:], fwd[:], RELU)
            r.append(rd)
        planes(nc.scalar.copy, y_wide, 0, 256, 0, "a")
        planes(nc.scalar.copy, y_wide, 256, 128, 256, "b")
        back = psum.tile([P, T], F32, name="back", tag="back", bufs=2)
        add_transposed(back, [(blk(t), r[d][:, blk(t)]) for d in range(2) for t in range(PACK)])
        pre = keep.tile([P, PACK, BLK], F32, name="prel")
        y_last = keep.tile([P, PACK, BLK], F32, name="y_last")
        back_t = back[:].rearrange("p (t c) -> p t c", t=PACK)
        for t0, t1 in ((0, 3), (3, 4)):
            nc.vector.tensor_tensor(pre[:, t0:t1], u[2][:, t0:t1], s[:, t0:t1, WIDE:T], ALU.add)
        for t0, t1 in ((0, 3), (3, 4)):
            nc.vector.scalar_tensor_tensor(y_last[:, t0:t1], pre[:, t0:t1], 0.0, back_t[:, t0:t1], ALU.max, ALU.add)
        nc.sync.dma_start(out=out_rows[:, :, WIDE:T], in_=y_last[:])
        planes(nc.vector.tensor_copy, y_last, 0, BLK, WIDE, "c")
        for q in range(4):
            queue = nc.scalar if q % 2 else nc.sync
            queue.dma_start(out=out_2[0, 4 * q : 4 * q + 4, :].bitcast(I32), in_=y_sc[32 * q : 32 * q + 4, :].bitcast(I32))
